import numpy as np
import ml_dtypes


def mxq(x, axis, fmt="e4m3"):
    dtype, down = {"e4m3": (ml_dtypes.float8_e4m3fn, 7), "e5m2": (ml_dtypes.float8_e5m2, 14)}[fmt]
    v = np.moveaxis(np.asarray(x, np.float32).astype(ml_dtypes.bfloat16).astype(np.float64), axis, -1)
    blocks = v.reshape(v.shape[:-1] + (-1, 32))
    amax = np.abs(blocks).max(-1, keepdims=True)
    byte = np.maximum(np.where(amax > 0, np.frexp(amax)[1] - 1 + 127, 0) - down, 1)
    scale = np.exp2(byte - 127.0)
    codes = (blocks / scale).astype(np.float32).astype(dtype).astype(np.float64)
    return np.moveaxis((codes * scale).reshape(v.shape), -1, axis)


WIDE = False


def mx_kscale(k):
    if not WIDE:
        return np.ones(k)
    levels = np.array([10, -10, 5, -5, 0])
    if k % 512:
        return np.exp2(np.random.permutation(np.resize(levels, k // 32))).repeat(32)
    a = np.empty((k // 512, 16))
    for p in range(k // 512):
        a[p, :8] = np.random.permutation(np.resize(levels, 8))
        for g in range(8):
            far = levels[np.abs(levels - a[p, g]) >= 10]
            a[p, g + 8] = far[np.random.randint(len(far))]
    return np.exp2(a.ravel()).repeat(32)


def f64(x):
    return np.asarray(x).astype(np.float64)


def striped(idx):
    return np.tile(idx.reshape(-1, 16).T, (8, 1)).astype(np.uint16)


def unstriped(offs):
    return offs[:16].T.reshape(-1).astype(np.int64)


def striped8(idx):
    return np.concatenate([x.reshape(-1, 16).T for x in idx]).astype(np.uint16)


def runs(offs, k):
    lists = np.stack([offs[16 * r : 16 * r + 16].T.reshape(-1) for r in range(8)]).astype(np.int64)
    return lists[np.arange(k) % 512 // 64]


def pack_weight(w):
    k, n = w.shape
    w = f64(np.asarray(w, np.float32).astype(ml_dtypes.bfloat16)).reshape(k // 32, 32, n)
    amax = np.abs(w).max(1)
    byte = np.clip(np.where(amax > 0, np.frexp(amax)[1] - 1 + 127 - 7, 1), 1, 254)
    scaled = (w * np.exp2(127.0 - byte)[:, None, :]).reshape(k, n).astype(np.float32)
    words = np.ascontiguousarray(scaled.reshape(k // 512, 128, 4, n).transpose(0, 1, 3, 2)).astype(ml_dtypes.float8_e4m3fn).view(np.uint8)
    return words, np.ascontiguousarray(byte.astype(np.uint8).reshape(k // 512, 16, n))


def unpack_weight(words, scales):
    g, p, n, _ = words.shape
    vals = np.ascontiguousarray(words).view(ml_dtypes.float8_e4m3fn).astype(np.float64) * np.repeat(np.exp2(scales.astype(np.float64) - 127.0), 8, axis=1)[..., None]
    return vals.transpose(0, 1, 3, 2).reshape(g * 512, n)


def relu(v):
    return np.maximum(v, 0.0)


K, T, S, N, H, W, U = 512, 2048, 512, 512, 512, 256, 1024


def setup_inputs():
    n = np.random.standard_normal
    s = mx_kscale(K)[:, None]
    u = mx_kscale(S)
    packed_xT = pack_weight(n((K, T)) * s)
    perm = np.stack([np.random.permutation(H) for _ in range(8)])
    return {
        "x_words": packed_xT[0],
        "x_scales": packed_xT[1],
        "wa": (n((K, H)) / np.sqrt(K) / s).astype(np.float32),
        "wb": (n((K, N)) / np.sqrt(K) / s).astype(np.float32),
        "gt": (np.random.uniform(0.5, 1.5, (S, 1)) * u[:, None]).astype(np.float32),
        "gi": (np.random.uniform(0.5, 1.5, (S, 1)) / u[:, None]).astype(np.float32),
        "offs": striped(np.random.permutation(T)[:S]),
        "two": striped(np.random.permutation(T)[:S]),
        "n1": striped8(perm[:, :W]),
        "n2": striped8(perm[:, W:]),
        "n3": striped8(np.stack([np.random.permutation(H) for _ in range(8)])),
        "n4": striped8(np.stack([np.random.permutation(U)[:N] for _ in range(8)])),
        "n5": striped8(np.stack([np.random.permutation(N) for _ in range(8)])),
    }


def reference(x_words, x_scales, wa, wb, gt, gi, offs, two, n1, n2, n3, n4, n5):
    xq = unpack_weight(x_words, x_scales)[:, unstriped(offs)]
    a = xq.T @ mxq(f64(wa), 0, "e4m3")
    pa = a[np.arange(S)[:, None], runs(n1, S)]
    pb = a[np.arange(S)[:, None], runs(n2, S)]
    ra = pa - (0.5 * pb)
    ds = a.copy()
    ds[np.arange(S)[:, None], runs(n2, S)] = ra
    z = f64(gt) * (ds - (0.5 * (ds[np.arange(S)[:, None], runs(n3, S)])))
    x_two = unpack_weight(x_words, x_scales)[:, unstriped(two)]
    b = x_two.T @ mxq(f64(wb), 0, "e4m3")
    z2 = f64(gi) * b
    cv = 0.0625 * ((mxq(z, 0, "e4m3").T @ mxq(z2, 0, "e4m3")))
    nw = cv - (relu(cv[np.arange(H)[:, None], runs(n5, H)]))
    out = np.zeros((H, U))
    out[np.arange(H)[:, None], runs(n4, H)] = nw
    return out

@@ -1,0 +1,233 @@
+from contextlib import ExitStack
+
+import concourse.mybir as mybir
+
+F32 = mybir.dt.float32
+BF16 = mybir.dt.bfloat16
+I32 = mybir.dt.int32
+U32 = mybir.dt.uint32
+U16 = mybir.dt.uint16
+U8 = mybir.dt.uint8
+FP8X4 = mybir.dt.float8_e4m3fn_x4
+ALU = mybir.AluOpType
+ACT = mybir.ActivationFunctionType
+
+P = 128
+PACK = 4
+T, S, H, N, W, U = 2048, 512, 512, 512, 256, 1024
+WA_CHUNKS = ((0, 256), (256, 128), (384, 128))
+FLOPS = 3 * 2 * 512 * 512 * 512
+
+
+def tile_picked_momfolddpagez_none_p_kernel(tc, x_words, x_scales, wa, wb, gt, gi, offs, two, n1, n2, n3, n4, n5, out):
+    nc = tc.nc
+    with ExitStack() as ctx:
+        keep = ctx.enter_context(tc.tile_pool(name="keep", bufs=1))
+        psum = ctx.enter_context(tc.psum_pool(name="psum", bufs=1))
+
+        def sb(shape, dtype, name):
+            return keep.tile(shape, dtype, name=name, align_bytes=64)
+
+        def load_list(src, name):
+            tile = keep.tile(list(src.shape), U16, name=name)
+            nc.sync.dma_start(tile[:], src)
+            return tile
+
+        def load_weight(src, c0, width, name):
+            raw = sb([P, PACK, width], F32, name)
+            nc.sync.dma_start(raw[:], src.rearrange("(p j) c -> p j c", j=PACK)[:, :, c0 : c0 + width])
+            return raw
+
+        def load_rows(src, name):
+            tile = sb([P, PACK], F32, name)
+            nc.sync.dma_start(tile[:], src.rearrange("(p t) o -> p (t o)", t=PACK))
+            return tile
+
+        xs = sb([P, T], U8, "xs")
+        nc.vector.memset(xs[:].bitcast(I32), 0)
+        for q in range(4):
+            nc.scalar.dma_start(xs[32 * q : 32 * q + 4, :].bitcast(I32), x_scales[0, 4 * q : 4 * q + 4, :].bitcast(I32))
+        offs_sb = load_list(offs, "offs_sb")
+        wa_raw = [load_weight(wa, *WA_CHUNKS[0], "wa_raw0")]
+        xw = sb([P, T], I32, "xw")
+        nc.sync.dma_start(xw[:], x_words[0].rearrange("p n t -> p (n t)").bitcast(I32))
+        two_sb = load_list(two, "two_sb")
+        wa_raw.append(load_weight(wa, *WA_CHUNKS[1], "wa_raw1"))
+        wa_raw.append(load_weight(wa, *WA_CHUNKS[2], "wa_raw2"))
+        gt_sb = load_rows(gt, "gt_sb")
+        n1_sb = load_list(n1, "n1_sb")
+        n2_sb = load_list(n2, "n2_sb")
+        wb_raw = [load_weight(wb, c0, 256, "wb_raw%d" % c0) for c0 in (0, 256)]
+        gi_sb = load_rows(gi, "gi_sb")
+        n3_sb = load_list(n3, "n3_sb")
+        n5_sb = load_list(n5, "n5_sb")
+        n4_sb = load_list(n4, "n4_sb")
+
+        rows = [sb([P, 2 * H], F32, "rows%d" % t) for t in range(PACK)]
+        page = [sb([P, U], F32, "page%d" % t) for t in range(PACK)]
+        for t in range(PACK):
+            nc.vector.memset(rows[t][:, H:], 0.0)
+        for t in range(PACK):
+            nc.gpsimd.memset(page[t][:], 0.0)
+
+        def pick_scales(lst, name):
+            picked = sb([P, S], U8, name + "_picked")
+            nc.vector.tensor_copy(picked[:], xs[:].indirect(lst[:]))
+            dealt = sb([P, PACK, P], U8, name)
+            return picked, dealt
+
+        def deal_scales(picked, dealt):
+            nc.vector.tensor_copy(dealt[:], picked[:].rearrange("p (m t) -> p t m", t=PACK))
+
+        def pick_words(lst, name):
+            dealt = sb([P, PACK, P], U32, name)
+            nc.vector.tensor_copy(dealt[:].rearrange("p t m -> p m t"), xw[:].bitcast(U32).indirect(lst[:]))
+            return dealt
+
+        def cast_weight(raw, width, name):
+            grouped = sb([P, width, PACK], BF16, name)
+            nc.scalar.copy(
+                grouped[:].rearrange("p (c i) j -> p c j i", i=4),
+                raw[:].rearrange("p j (c i) -> p c j i", i=4),
+            )
+            return grouped
+
+        def quantize(grouped_ap, width, name):
+            codes = sb([P, width], U32, name + "_codes")
+            scales = sb([P, width], U8, name + "_scales")
+            nc.vector.quantize_mx(out=codes[:].bitcast(FP8X4), scales=scales[:], in_=grouped_ap)
+            return codes, scales
+
+        def product(acc, lhs, rhs):
+            nc.tensor.matmul_mx(
+                out=acc,
+                lhsT=lhs[0].bitcast(FP8X4),
+                lhsT_scale=lhs[1],
+                rhs=rhs[0].bitcast(FP8X4),
+                rhs_scale=rhs[1],
+                start=True,
+                stop=True,
+            )
+
+        pa_s, xa_s = pick_scales(offs_sb, "xa_s")
+        pb_s, xb_s = pick_scales(two_sb, "xb_s")
+        deal_scales(pa_s, xa_s)
+        deal_scales(pb_s, xb_s)
+
+        wa_q = []
+        xa_w = None
+        for i, (c0, width) in enumerate(WA_CHUNKS):
+            grouped = cast_weight(wa_raw[i], width, "wa_bf%d" % i)
+            wa_q.append(quantize(grouped[:].rearrange("p c j -> p (c j)"), width, "wa%d" % i))
+            if i == 0:
+                xa_w = pick_words(offs_sb, "xa_w")
+        xb_w = pick_words(two_sb, "xb_w")
+
+        banks = [psum.tile([P, 512], F32, name="bank%d" % i) for i in range(8)]
+        a_at = {}
+        for t in range(PACK):
+            a_at[(0, t)] = banks[t // 2][:, (t % 2) * 256 : (t % 2 + 1) * 256]
+            a_at[(1, t)] = banks[2][:, t * 128 : (t + 1) * 128]
+            a_at[(2, t)] = banks[3][:, t * 128 : (t + 1) * 128]
+        for i in range(len(WA_CHUNKS)):
+            for t in range(PACK):
+                product(a_at[(i, t)], (xa_w[:, t, :], xa_s[:, t, :]), (wa_q[i][0][:], wa_q[i][1][:]))
+        for t in range(PACK):
+            for i, (c0, width) in enumerate(WA_CHUNKS):
+                nc.scalar.activation(rows[t][:, c0 : c0 + width], a_at[(i, t)], ACT.Copy, scale=gt_sb[:, t : t + 1])
+
+        pa = sb([P, PACK, W], F32, "pa")
+        pb = sb([P, PACK, W], F32, "pb")
+        twice = sb([P, PACK, H], F32, "twice")
+        y = sb([P, PACK, H], F32, "y")
+
+        def fetch_pairs(t):
+            nc.vector.tensor_copy(pa[:, t, :], rows[t][:].indirect(n1_sb[:]))
+            nc.vector.tensor_scalar(pb[:, t, :], rows[t][:].indirect(n2_sb[:]), -0.5, 0.0, ALU.mult, ALU.add)
+
+        def put_back(t):
+            nc.vector.tensor_tensor(rows[t][:].indirect(n2_sb[:]), pa[:, t, :], pb[:, t, :], ALU.add)
+            nc.scalar.activation(twice[:, t, :], rows[t][:, :H], ACT.Copy, scale=2.0)
+
+        def fold(t):
+            nc.vector.tensor_tensor(y[:, t, :], rows[t][:].indirect(n3_sb[:]), twice[:, t, :], ALU.subtract)
+
+        z_bf = sb([P, PACK, P, PACK], BF16, "z_bf")
+        z2_planes = sb([P, PACK, N], BF16, "z2_planes")
+        z2_bf = sb([P, N, PACK], BF16, "z2_bf")
+
+        wb_codes = sb([P, N], U32, "wb_codes")
+        wb_scales = sb([P, N], U8, "wb_scales")
+
+        fetch_pairs(0)
+        fetch_pairs(1)
+        put_back(0)
+        wb_bf = [cast_weight(wb_raw[i], 256, "wb_bf%d" % i) for i in range(2)]
+        fetch_pairs(2)
+        put_back(1)
+        for i in range(2):
+            nc.vector.quantize_mx(
+                out=wb_codes[:, i * 256 : (i + 1) * 256].bitcast(FP8X4),
+                scales=wb_scales[:, i * 256 : (i + 1) * 256],
+                in_=wb_bf[i][:].rearrange("p c j -> p (c j)"),
+            )
+        fold(0)
+        for t in range(PACK):
+            product(banks[4 + t][:], (xb_w[:, t, :], xb_s[:, t, :]), (wb_codes[:], wb_scales[:]))
+            nc.scalar.activation(z2_planes[:, t, :], banks[4 + t][:], ACT.Copy, scale=gi_sb[:, t : t + 1])
+        fetch_pairs(3)
+        put_back(2)
+        fold(1)
+        put_back(3)
+        for h in range(2):
+            nc.scalar.copy(
+                z2_bf[:, h * 256 : (h + 1) * 256, :].rearrange("p (c i) t -> p c t i", i=4),
+                z2_planes[:, :, h * 256 : (h + 1) * 256].rearrange("p t (c i) -> p c t i", i=4),
+            )
+        nc.scalar.activation(
+            z_bf[:, :, :, 0:2].rearrange("p u m t -> p m u t"),
+            y[:, 0:2, :].rearrange("p t (m u) -> p m u t", u=PACK),
+            ACT.Copy,
+            scale=-0.5,
+        )
+        fold(2)
+        fold(3)
+        z2_q = quantize(z2_bf[:].rearrange("p n t -> p (n t)"), N, "z2")
+
+        cv = sb([P, PACK, N], F32, "cv")
+        neg = sb([P, PACK, N], F32, "neg")
+        out_rows = out.rearrange("(p u) w -> u p w", u=PACK)
+
+        def moments(u):
+            nc.scalar.activation(
+                z_bf[:, u, :, 2:4],
+                y[:, 2:4, :].rearrange("p t (m u) -> p u m t", u=PACK)[:, u, :, :],
+                ACT.Copy,
+                scale=-0.5,
+            )
+            z_q = quantize(z_bf[:, u, :, :].rearrange("p m t -> p (m t)"), P, "zblock%d" % u)
+            product(banks[u][:], (z_q[0][:], z_q[1][:]), (z2_q[0][:], z2_q[1][:]))
+
+        def leave(u):
+            nc.scalar.activation(rows[u][:, :N], banks[u][:], ACT.Relu, scale=0.0625)
+            nc.scalar.activation(cv[:, u, :], banks[u][:], ACT.Copy, scale=0.0625)
+
+        def fetch_relu(u):
+            nc.vector.tensor_scalar(neg[:, u, :], rows[u][:].indirect(n5_sb[:]), -1.0, 0.0, ALU.mult, ALU.add)
+
+        def put_page(u):
+            nc.vector.tensor_tensor(page[u][:].indirect(n4_sb[:]), cv[:, u, :], neg[:, u, :], ALU.add)
+            nc.sync.dma_start(out_rows[u], page[u][:])
+
+        moments(0)
+        moments(1)
+        leave(0)
+        moments(2)
+        moments(3)
+        for u in range(1, PACK):
+            leave(u)
+        fetch_relu(0)
+        for u in range(PACK):
+            if u + 1 < PACK:
+                fetch_relu(u + 1)
+            put_page(u)

@@ -25,8 +25,8 @@ def tile_picked_momfolddpagez_none_p_kernel(tc, x_words, x_scales, wa, wb, gt, g
         keep = ctx.enter_context(tc.tile_pool(name="keep", bufs=1))
         psum = ctx.enter_context(tc.psum_pool(name="psum", bufs=1))
 
-        def sb(shape, dtype, name):
-            return keep.tile(shape, dtype, name=name, align_bytes=64)
+        def sb(shape, dtype, name, tag=None):
+            return keep.tile(shape, dtype, name=name, tag=tag or name, align_bytes=64)
 
         def load_list(src, name):
             tile = keep.tile(list(src.shape), U16, name=name)
@@ -44,14 +44,14 @@ def tile_picked_momfolddpagez_none_p_kernel(tc, x_words, x_scales, wa, wb, gt, g
             return tile
 
         xs = sb([P, T], U8, "xs")
-        nc.vector.memset(xs[:].bitcast(I32), 0)
-        for q in range(4):
-            nc.scalar.dma_start(xs[32 * q : 32 * q + 4, :].bitcast(I32), x_scales[0, 4 * q : 4 * q + 4, :].bitcast(I32))
+        nc.gpsimd.memset(xs[:].bitcast(I32), 0)
         offs_sb = load_list(offs, "offs_sb")
         wa_raw = [load_weight(wa, *WA_CHUNKS[0], "wa_raw0")]
+        for q in range(4):
+            nc.sync.dma_start(xs[32 * q : 32 * q + 4, :].bitcast(I32), x_scales[0, 4 * q : 4 * q + 4, :].bitcast(I32))
+        two_sb = load_list(two, "two_sb")
         xw = sb([P, T], I32, "xw")
         nc.sync.dma_start(xw[:], x_words[0].rearrange("p n t -> p (n t)").bitcast(I32))
-        two_sb = load_list(two, "two_sb")
         wa_raw.append(load_weight(wa, *WA_CHUNKS[1], "wa_raw1"))
         wa_raw.append(load_weight(wa, *WA_CHUNKS[2], "wa_raw2"))
         gt_sb = load_rows(gt, "gt_sb")
@@ -66,9 +66,7 @@ def tile_picked_momfolddpagez_none_p_kernel(tc, x_words, x_scales, wa, wb, gt, g
         rows = [sb([P, 2 * H], F32, "rows%d" % t) for t in range(PACK)]
         page = [sb([P, U], F32, "page%d" % t) for t in range(PACK)]
         for t in range(PACK):
-            nc.vector.memset(rows[t][:, H:], 0.0)
-        for t in range(PACK):
-            nc.gpsimd.memset(page[t][:], 0.0)
+            (nc.vector if t < 2 else nc.gpsimd).memset(page[t][:], 0.0)
 
         def pick_scales(lst, name):
             picked = sb([P, S], U8, name + "_picked")
@@ -84,16 +82,14 @@ def tile_picked_momfolddpagez_none_p_kernel(tc, x_words, x_scales, wa, wb, gt, g
             nc.vector.tensor_copy(dealt[:].rearrange("p t m -> p m t"), xw[:].bitcast(U32).indirect(lst[:]))
             return dealt
 
-        def cast_weight(raw, width, name):
-            grouped = sb([P, width, PACK], BF16, name)
+        def cast_weight(raw, grouped):
             nc.scalar.copy(
-                grouped[:].rearrange("p (c i) j -> p c j i", i=4),
+                grouped.rearrange("p (c i) j -> p c j i", i=4),
                 raw[:].rearrange("p j (c i) -> p c j i", i=4),
             )
-            return grouped
 
-        def quantize(grouped_ap, width, name):
-            codes = sb([P, width], U32, name + "_codes")
+        def quantize(grouped_ap, width, name, tag=None):
+            codes = sb([P, width], U32, name + "_codes", tag)
             scales = sb([P, width], U8, name + "_scales")
             nc.vector.quantize_mx(out=codes[:].bitcast(FP8X4), scales=scales[:], in_=grouped_ap)
             return codes, scales
@@ -117,7 +113,8 @@ def tile_picked_momfolddpagez_none_p_kernel(tc, x_words, x_scales, wa, wb, gt, g
         wa_q = []
         xa_w = None
         for i, (c0, width) in enumerate(WA_CHUNKS):
-            grouped = cast_weight(wa_raw[i], width, "wa_bf%d" % i)
+            grouped = sb([P, width, PACK], BF16, "wa_bf%d" % i)
+            cast_weight(wa_raw[i], grouped[:])
             wa_q.append(quantize(grouped[:].rearrange("p c j -> p (c j)"), width, "wa%d" % i))
             if i == 0:
                 xa_w = pick_words(offs_sb, "xa_w")
@@ -132,67 +129,74 @@ def tile_picked_momfolddpagez_none_p_kernel(tc, x_words, x_scales, wa, wb, gt, g
         for i in range(len(WA_CHUNKS)):
             for t in range(PACK):
                 product(a_at[(i, t)], (xa_w[:, t, :], xa_s[:, t, :]), (wa_q[i][0][:], wa_q[i][1][:]))
-        for t in range(PACK):
-            for i, (c0, width) in enumerate(WA_CHUNKS):
+        for i, (c0, width) in enumerate(WA_CHUNKS):
+            for t in range(PACK):
                 nc.scalar.activation(rows[t][:, c0 : c0 + width], a_at[(i, t)], ACT.Copy, scale=gt_sb[:, t : t + 1])
 
-        pa = sb([P, PACK, W], F32, "pa")
-        pb = sb([P, PACK, W], F32, "pb")
-        twice = sb([P, PACK, H], F32, "twice")
+        twice = {}
         y = sb([P, PACK, H], F32, "y")
+        pairs = {}
 
         def fetch_pairs(t):
-            nc.vector.tensor_copy(pa[:, t, :], rows[t][:].indirect(n1_sb[:]))
-            nc.vector.tensor_scalar(pb[:, t, :], rows[t][:].indirect(n2_sb[:]), -0.5, 0.0, ALU.mult, ALU.add)
+            held = pairs[t // 2]
+            nc.vector.tensor_copy(held[:, t % 2, 0, :], rows[t][:].indirect(n1_sb[:]))
+            nc.vector.tensor_scalar(held[:, t % 2, 1, :], rows[t][:].indirect(n2_sb[:]), -0.5, 0.0, ALU.mult, ALU.add)
 
         def put_back(t):
-            nc.vector.tensor_tensor(rows[t][:].indirect(n2_sb[:]), pa[:, t, :], pb[:, t, :], ALU.add)
-            nc.scalar.activation(twice[:, t, :], rows[t][:, :H], ACT.Copy, scale=2.0)
+            held = pairs[t // 2]
+            nc.vector.tensor_tensor(rows[t][:].indirect(n2_sb[:]), held[:, t % 2, 0, :], held[:, t % 2, 1, :], ALU.add)
+
+        def double(t):
+            nc.scalar.activation(twice[t], rows[t][:, :H], ACT.Copy, scale=2.0)
 
         def fold(t):
-            nc.vector.tensor_tensor(y[:, t, :], rows[t][:].indirect(n3_sb[:]), twice[:, t, :], ALU.subtract)
+            nc.vector.tensor_tensor(y[:, t, :], rows[t][:].indirect(n3_sb[:]), twice[t], ALU.subtract)
 
         z_bf = sb([P, PACK, P, PACK], BF16, "z_bf")
         z2_planes = sb([P, PACK, N], BF16, "z2_planes")
         z2_bf = sb([P, N, PACK], BF16, "z2_bf")
 
-        wb_codes = sb([P, N], U32, "wb_codes")
-        wb_scales = sb([P, N], U8, "wb_scales")
-
+        wb_bf = sb([P, N, PACK], BF16, "wb_bf")
+        for i in range(2):
+            cast_weight(wb_raw[i], wb_bf[:, i * 256 : (i + 1) * 256, :])
+        pairs[0] = sb([P, 2, 2, W], F32, "pairs0")
         fetch_pairs(0)
         fetch_pairs(1)
         put_back(0)
-        wb_bf = [cast_weight(wb_raw[i], 256, "wb_bf%d" % i) for i in range(2)]
-        fetch_pairs(2)
         put_back(1)
-        for i in range(2):
-            nc.vector.quantize_mx(
-                out=wb_codes[:, i * 256 : (i + 1) * 256].bitcast(FP8X4),
-                scales=wb_scales[:, i * 256 : (i + 1) * 256],
-                in_=wb_bf[i][:].rearrange("p c j -> p (c j)"),
-            )
-        fold(0)
+        wb_q = quantize(wb_bf[:].rearrange("p c j -> p (c j)"), N, "wb")
+        twice01 = sb([P, 2, H], F32, "twice01", "wb_raw256")
+        twice[0], twice[1] = twice01[:, 0, :], twice01[:, 1, :]
+        twice[2] = sb([P, H], F32, "twice2")[:]
+        twice[3] = sb([P, H], F32, "twice3")[:]
+        double(0)
+        double(1)
         for t in range(PACK):
-            product(banks[4 + t][:], (xb_w[:, t, :], xb_s[:, t, :]), (wb_codes[:], wb_scales[:]))
+            product(banks[4 + t][:], (xb_w[:, t, :], xb_s[:, t, :]), (wb_q[0][:], wb_q[1][:]))
             nc.scalar.activation(z2_planes[:, t, :], banks[4 + t][:], ACT.Copy, scale=gi_sb[:, t : t + 1])
-        fetch_pairs(3)
-        put_back(2)
-        fold(1)
-        put_back(3)
         for h in range(2):
             nc.scalar.copy(
                 z2_bf[:, h * 256 : (h + 1) * 256, :].rearrange("p (c i) t -> p c t i", i=4),
                 z2_planes[:, :, h * 256 : (h + 1) * 256].rearrange("p t (c i) -> p c t i", i=4),
             )
+        pairs[1] = sb([P, 2, 2, W], F32, "pairs1", "wb_bf")
+        fetch_pairs(2)
+        fold(0)
+        fetch_pairs(3)
+        put_back(2)
+        double(2)
+        fold(1)
         nc.scalar.activation(
             z_bf[:, :, :, 0:2].rearrange("p u m t -> p m u t"),
             y[:, 0:2, :].rearrange("p t (m u) -> p m u t", u=PACK),
             ACT.Copy,
             scale=-0.5,
         )
+        put_back(3)
+        double(3)
         fold(2)
         fold(3)
-        z2_q = quantize(z2_bf[:].rearrange("p n t -> p (n t)"), N, "z2")
+        z2_q = quantize(z2_bf[:].rearrange("p n t -> p (n t)"), N, "z2", "twice3")
 
         cv = sb([P, PACK, N], F32, "cv")
         neg = sb([P, PACK, N], F32, "neg")
@@ -208,8 +212,13 @@ def tile_picked_momfolddpagez_none_p_kernel(tc, x_words, x_scales, wa, wb, gt, g
             z_q = quantize(z_bf[:, u, :, :].rearrange("p m t -> p (m t)"), P, "zblock%d" % u)
             product(banks[u][:], (z_q[0][:], z_q[1][:]), (z2_q[0][:], z2_q[1][:]))
 
+        def positive(u):
+            if u == 0:
+                nc.vector.tensor_scalar(rows[u][:, :N], banks[u][:], 0.0625, 0.0, ALU.mult, ALU.max)
+            else:
+                nc.scalar.activation(rows[u][:, :N], banks[u][:], ACT.Relu, scale=0.0625)
+
         def leave(u):
-            nc.scalar.activation(rows[u][:, :N], banks[u][:], ACT.Relu, scale=0.0625)
             nc.scalar.activation(cv[:, u, :], banks[u][:], ACT.Copy, scale=0.0625)
 
         def fetch_relu(u):
@@ -221,13 +230,13 @@ def tile_picked_momfolddpagez_none_p_kernel(tc, x_words, x_scales, wa, wb, gt, g
 
         moments(0)
         moments(1)
-        leave(0)
-        moments(2)
-        moments(3)
-        for u in range(1, PACK):
-            leave(u)
+        positive(0)
         fetch_relu(0)
         for u in range(PACK):
             if u + 1 < PACK:
+                positive(u + 1)
                 fetch_relu(u + 1)
+            if u + 2 < PACK:
+                moments(u + 2)
+            leave(u)
             put_page(u)

@@ -1,6 +1,7 @@
 from contextlib import ExitStack
 
 import concourse.mybir as mybir
+from concourse.masks import make_identity
 
 F32 = mybir.dt.float32
 BF16 = mybir.dt.bfloat16
@@ -15,7 +16,8 @@ ACT = mybir.ActivationFunctionType
 P = 128
 PACK = 4
 T, S, H, N, W, U = 2048, 512, 512, 512, 256, 1024
-WA_CHUNKS = ((0, 256), (256, 128), (384, 128))
+HALF = 256
+RUN = 8
 FLOPS = 3 * 2 * 512 * 512 * 512
 
 
@@ -38,27 +40,33 @@ def tile_picked_momfolddpagez_none_p_kernel(tc, x_words, x_scales, wa, wb, gt, g
             nc.sync.dma_start(raw[:], src.rearrange("(p j) c -> p j c", j=PACK)[:, :, c0 : c0 + width])
             return raw
 
-        def load_rows(src, name):
-            tile = sb([P, PACK], F32, name)
-            nc.sync.dma_start(tile[:], src.rearrange("(p t) o -> p (t o)", t=PACK))
+        def load_gate(src, queue, name):
+            tile = sb([P, P], F32, name)
+            nc.gpsimd.memset(tile[:], 0.0)
+            queue.dma_start(
+                tile[:PACK, :].rearrange("t (b i) -> t b i", i=RUN),
+                src.rearrange("(b t i) o -> t b (i o)", t=PACK, i=RUN),
+            )
             return tile
 
         xs = sb([P, T], U8, "xs")
-        nc.gpsimd.memset(xs[:].bitcast(I32), 0)
+        nc.vector.memset(xs[:].bitcast(I32), 0)
+        gt_rows = load_gate(gt, nc.gpsimd, "gt_rows")
+        ident = sb([P, P], F32, "ident")
+        make_identity(nc, ident[:])
+
         offs_sb = load_list(offs, "offs_sb")
-        wa_raw = [load_weight(wa, *WA_CHUNKS[0], "wa_raw0")]
+        wa_raw = [load_weight(wa, 0, HALF, "wa_raw0")]
         for q in range(4):
             nc.sync.dma_start(xs[32 * q : 32 * q + 4, :].bitcast(I32), x_scales[0, 4 * q : 4 * q + 4, :].bitcast(I32))
         two_sb = load_list(two, "two_sb")
+        wa_raw.append(load_weight(wa, HALF, HALF, "wa_raw1"))
         xw = sb([P, T], I32, "xw")
         nc.sync.dma_start(xw[:], x_words[0].rearrange("p n t -> p (n t)").bitcast(I32))
-        wa_raw.append(load_weight(wa, *WA_CHUNKS[1], "wa_raw1"))
-        wa_raw.append(load_weight(wa, *WA_CHUNKS[2], "wa_raw2"))
-        gt_sb = load_rows(gt, "gt_sb")
         n1_sb = load_list(n1, "n1_sb")
         n2_sb = load_list(n2, "n2_sb")
-        wb_raw = [load_weight(wb, c0, 256, "wb_raw%d" % c0) for c0 in (0, 256)]
-        gi_sb = load_rows(gi, "gi_sb")
+        wb_raw = [load_weight(wb, c0, HALF, "wb_raw%d" % c0) for c0 in (0, HALF)]
+        gi_rows = load_gate(gi, nc.sync, "gi_rows")
         n3_sb = load_list(n3, "n3_sb")
         n5_sb = load_list(n5, "n5_sb")
         n4_sb = load_list(n4, "n4_sb")
@@ -71,15 +79,18 @@ def tile_picked_momfolddpagez_none_p_kernel(tc, x_words, x_scales, wa, wb, gt, g
         def pick_scales(lst, name):
             picked = sb([P, S], U8, name + "_picked")
             nc.vector.tensor_copy(picked[:], xs[:].indirect(lst[:]))
-            dealt = sb([P, PACK, P], U8, name)
+            dealt = sb([P, S], U8, name)
             return picked, dealt
 
         def deal_scales(picked, dealt):
-            nc.vector.tensor_copy(dealt[:], picked[:].rearrange("p (m t) -> p t m", t=PACK))
+            nc.vector.tensor_copy(
+                dealt[:].bitcast(I32).rearrange("p (t b w) -> p t b w", t=PACK, w=RUN // 4),
+                picked[:].bitcast(I32).rearrange("p (b t w) -> p t b w", t=PACK, w=RUN // 4),
+            )
 
         def pick_words(lst, name):
             dealt = sb([P, PACK, P], U32, name)
-            nc.vector.tensor_copy(dealt[:].rearrange("p t m -> p m t"), xw[:].bitcast(U32).indirect(lst[:]))
+            nc.vector.tensor_copy(dealt[:].rearrange("p t (b i) -> p b t i", i=RUN), xw[:].bitcast(U32).indirect(lst[:]))
             return dealt
 
         def cast_weight(raw, grouped):
@@ -111,27 +122,30 @@ def tile_picked_momfolddpagez_none_p_kernel(tc, x_words, x_scales, wa, wb, gt, g
         deal_scales(pb_s, xb_s)
 
         wa_q = []
-        xa_w = None
-        for i, (c0, width) in enumerate(WA_CHUNKS):
-            grouped = sb([P, width, PACK], BF16, "wa_bf%d" % i)
-            cast_weight(wa_raw[i], grouped[:])
-            wa_q.append(quantize(grouped[:].rearrange("p c j -> p (c j)"), width, "wa%d" % i))
-            if i == 0:
-                xa_w = pick_words(offs_sb, "xa_w")
+        for h in range(2):
+            grouped = sb([P, HALF, PACK], BF16, "wa_bf%d" % h)
+            cast_weight(wa_raw[h], grouped[:])
+            wa_q.append(quantize(grouped[:].rearrange("p c j -> p (c j)"), HALF, "wa%d" % h))
+        xa_w = pick_words(offs_sb, "xa_w")
         xb_w = pick_words(two_sb, "xb_w")
 
         banks = [psum.tile([P, 512], F32, name="bank%d" % i) for i in range(8)]
-        a_at = {}
-        for t in range(PACK):
-            a_at[(0, t)] = banks[t // 2][:, (t % 2) * 256 : (t % 2 + 1) * 256]
-            a_at[(1, t)] = banks[2][:, t * 128 : (t + 1) * 128]
-            a_at[(2, t)] = banks[3][:, t * 128 : (t + 1) * 128]
-        for i in range(len(WA_CHUNKS)):
-            for t in range(PACK):
-                product(a_at[(i, t)], (xa_w[:, t, :], xa_s[:, t, :]), (wa_q[i][0][:], wa_q[i][1][:]))
-        for i, (c0, width) in enumerate(WA_CHUNKS):
-            for t in range(PACK):
-                nc.scalar.activation(rows[t][:, c0 : c0 + width], a_at[(i, t)], ACT.Copy, scale=gt_sb[:, t : t + 1])
+
+        def turn_gate(gate_rows, name):
+            tile = sb([P, PACK], F32, name)
+            nc.tensor.transpose(banks[7][:, :P], gate_rows[:], ident[:])
+            nc.scalar.copy(tile[:], banks[7][:, :PACK])
+            return tile
+
+        gt_sb = turn_gate(gt_rows, "gt_sb")
+
+        for t0 in (0, 2):
+            for h in range(2):
+                for t in (t0, t0 + 1):
+                    acc = banks[2 * t + h][:, :HALF]
+                    product(acc, (xa_w[:, t, :], xa_s[:, t * P : (t + 1) * P]), (wa_q[h][0][:], wa_q[h][1][:]))
+                    nc.scalar.activation(rows[t][:, h * HALF : (h + 1) * HALF], acc, ACT.Copy, scale=gt_sb[:, t : t + 1])
+        gi_sb = turn_gate(gi_rows, "gi_sb")
 
         twice = {}
         y = sb([P, PACK, H], F32, "y")
@@ -156,7 +170,7 @@ def tile_picked_momfolddpagez_none_p_kernel(tc, x_words, x_scales, wa, wb, gt, g
         z2_planes = sb([P, PACK, N], BF16, "z2_planes")
         z2_bf = sb([P, N, PACK], BF16, "z2_bf")
 
-        wb_bf = sb([P, N, PACK], BF16, "wb_bf")
+        wb_bf = sb([P, N, PACK], BF16, "wb_bf", "wa1_codes")
         for i in range(2):
             cast_weight(wb_raw[i], wb_bf[:, i * 256 : (i + 1) * 256, :])
         pairs[0] = sb([P, 2, 2, W], F32, "pairs0")
@@ -172,14 +186,14 @@ def tile_picked_momfolddpagez_none_p_kernel(tc, x_words, x_scales, wa, wb, gt, g
         double(0)
         double(1)
         for t in range(PACK):
-            product(banks[4 + t][:], (xb_w[:, t, :], xb_s[:, t, :]), (wb_q[0][:], wb_q[1][:]))
+            product(banks[4 + t][:], (xb_w[:, t, :], xb_s[:, t * P : (t + 1) * P]), (wb_q[0][:], wb_q[1][:]))
             nc.scalar.activation(z2_planes[:, t, :], banks[4 + t][:], ACT.Copy, scale=gi_sb[:, t : t + 1])
         for h in range(2):
             nc.scalar.copy(
                 z2_bf[:, h * 256 : (h + 1) * 256, :].rearrange("p (c i) t -> p c t i", i=4),
                 z2_planes[:, :, h * 256 : (h + 1) * 256].rearrange("p t (c i) -> p c t i", i=4),
             )
-        pairs[1] = sb([P, 2, 2, W], F32, "pairs1", "wb_bf")
+        pairs[1] = sb([P, 2, 2, W], F32, "pairs1", "wa1_codes")
         fetch_pairs(2)
         fold(0)
         fetch_pairs(3)
@@ -210,16 +224,27 @@ def tile_picked_momfolddpagez_none_p_kernel(tc, x_words, x_scales, wa, wb, gt, g
                 scale=-0.5,
             )
             z_q = quantize(z_bf[:, u, :, :].rearrange("p m t -> p (m t)"), P, "zblock%d" % u)
-            product(banks[u][:], (z_q[0][:], z_q[1][:]), (z2_q[0][:], z2_q[1][:]))
+            if u == 0:
+                for h in range(2):
+                    cols = slice(h * HALF, (h + 1) * HALF)
+                    product(banks[4 * h][:, cols], (z_q[0][:], z_q[1][:]), (z2_q[0][:, cols], z2_q[1][:, cols]))
+            else:
+                product(banks[u][:], (z_q[0][:], z_q[1][:]), (z2_q[0][:], z2_q[1][:]))
 
         def positive(u):
             if u == 0:
-                nc.vector.tensor_scalar(rows[u][:, :N], banks[u][:], 0.0625, 0.0, ALU.mult, ALU.max)
+                nc.scalar.activation(rows[u][:, :HALF], banks[0][:, :HALF], ACT.Relu, scale=0.0625)
+                nc.vector.tensor_scalar(rows[u][:, HALF:N], banks[4][:, HALF:], 0.0625, 0.0, ALU.mult, ALU.max)
             else:
                 nc.scalar.activation(rows[u][:, :N], banks[u][:], ACT.Relu, scale=0.0625)
 
         def leave(u):
-            nc.scalar.activation(cv[:, u, :], banks[u][:], ACT.Copy, scale=0.0625)
+            if u == 0:
+                for h in range(2):
+                    cols = slice(h * HALF, (h + 1) * HALF)
+                    nc.scalar.activation(cv[:, u, cols], banks[4 * h][:, cols], ACT.Copy, scale=0.0625)
+            else:
+                nc.scalar.activation(cv[:, u, :], banks[u][:], ACT.Copy, scale=0.0625)
 
         def fetch_relu(u):
             nc.vector.tensor_scalar(neg[:, u, :], rows[u][:].indirect(n5_sb[:]), -1.0, 0.0, ALU.mult, ALU.add)

@@ -166,6 +166,15 @@ def tile_picked_momfolddpagez_none_p_kernel(tc, x_words, x_scales, wa, wb, gt, g
         def fold(t):
             nc.vector.tensor_tensor(y[:, t, :], rows[t][:].indirect(n3_sb[:]), twice[t], ALU.subtract)
 
+        def double_half(t, h):
+            nc.scalar.activation(twice_last[h][:], rows[t][:, h * HALF : (h + 1) * HALF], ACT.Copy, scale=2.0)
+
+        def fold_half(t, h):
+            entries = n3_sb[:, h * HALF // 16 : (h + 1) * HALF // 16]
+            nc.vector.tensor_tensor(
+                y[:, t, h * HALF : (h + 1) * HALF], rows[t][:].indirect(entries), twice_last[h][:], ALU.subtract
+            )
+
         z_bf = sb([P, PACK, P, PACK], BF16, "z_bf")
         z2_planes = sb([P, PACK, N], BF16, "z2_planes")
         z2_bf = sb([P, N, PACK], BF16, "z2_bf")
@@ -173,16 +182,16 @@ def tile_picked_momfolddpagez_none_p_kernel(tc, x_words, x_scales, wa, wb, gt, g
         wb_bf = sb([P, N, PACK], BF16, "wb_bf", "wa1_codes")
         for i in range(2):
             cast_weight(wb_raw[i], wb_bf[:, i * 256 : (i + 1) * 256, :])
-        pairs[0] = sb([P, 2, 2, W], F32, "pairs0")
+        pairs[0] = sb([P, 2, 2, W], F32, "pairs0")[:]
         fetch_pairs(0)
         fetch_pairs(1)
         put_back(0)
         put_back(1)
         wb_q = quantize(wb_bf[:].rearrange("p c j -> p (c j)"), N, "wb")
-        twice01 = sb([P, 2, H], F32, "twice01", "wb_raw256")
-        twice[0], twice[1] = twice01[:, 0, :], twice01[:, 1, :]
+        late = sb([P, 4 * H], F32, "late", "wb_raw256")
+        twice[0], twice[1] = late[:, :H], late[:, H : 2 * H]
         twice[2] = sb([P, H], F32, "twice2")[:]
-        twice[3] = sb([P, H], F32, "twice3")[:]
+        twice_last = [sb([P, HALF], F32, "twice3_%d" % h) for h in range(2)]
         double(0)
         double(1)
         for t in range(PACK):
@@ -193,7 +202,7 @@ def tile_picked_momfolddpagez_none_p_kernel(tc, x_words, x_scales, wa, wb, gt, g
                 z2_bf[:, h * 256 : (h + 1) * 256, :].rearrange("p (c i) t -> p c t i", i=4),
                 z2_planes[:, :, h * 256 : (h + 1) * 256].rearrange("p t (c i) -> p c t i", i=4),
             )
-        pairs[1] = sb([P, 2, 2, W], F32, "pairs1", "wa1_codes")
+        pairs[1] = late[:, 2 * H :].rearrange("p (t s w) -> p t s w", t=2, s=2)
         fetch_pairs(2)
         fold(0)
         fetch_pairs(3)
@@ -207,42 +216,48 @@ def tile_picked_momfolddpagez_none_p_kernel(tc, x_words, x_scales, wa, wb, gt, g
             scale=-0.5,
         )
         put_back(3)
-        double(3)
+        double_half(3, 0)
+        double_half(3, 1)
         fold(2)
-        fold(3)
-        z2_q = quantize(z2_bf[:].rearrange("p n t -> p (n t)"), N, "z2", "twice3")
+        z2_q = []
+        for h, done_with in ((0, "twice2"), (1, "twice3_0")):
+            fold_half(3, h)
+            z2_half = z2_bf[:, h * HALF : (h + 1) * HALF, :].rearrange("p n t -> p (n t)")
+            z2_q.append(quantize(z2_half, HALF, "z2_%d" % h, done_with))
 
         cv = sb([P, PACK, N], F32, "cv")
         neg = sb([P, PACK, N], F32, "neg")
         out_rows = out.rearrange("(p u) w -> u p w", u=PACK)
 
+        def moment_at(u, h):
+            bank = banks[4] if (u, h) == (0, 1) else banks[u]
+            return bank[:, h * HALF : (h + 1) * HALF]
+
         def moments(u):
-            nc.scalar.activation(
-                z_bf[:, u, :, 2:4],
-                y[:, 2:4, :].rearrange("p t (m u) -> p u m t", u=PACK)[:, u, :, :],
-                ACT.Copy,
-                scale=-0.5,
-            )
+            pieces = 2 if u < 2 else 1
+            for h in range(pieces):
+                ms = slice(h * P // pieces, (h + 1) * P // pieces)
+                nc.scalar.activation(
+                    z_bf[:, u, ms, 2:4],
+                    y[:, 2:4, :].rearrange("p t (m u) -> p u m t", u=PACK)[:, u, ms, :],
+                    ACT.Copy,
+                    scale=-0.5,
+                )
             z_q = quantize(z_bf[:, u, :, :].rearrange("p m t -> p (m t)"), P, "zblock%d" % u)
-            if u == 0:
-                for h in range(2):
-                    cols = slice(h * HALF, (h + 1) * HALF)
-                    product(banks[4 * h][:, cols], (z_q[0][:], z_q[1][:]), (z2_q[0][:, cols], z2_q[1][:, cols]))
-            else:
-                product(banks[u][:], (z_q[0][:], z_q[1][:]), (z2_q[0][:], z2_q[1][:]))
+            for h in range(2):
+                product(moment_at(u, h), (z_q[0][:], z_q[1][:]), (z2_q[h][0][:], z2_q[h][1][:]))
 
         def positive(u):
             if u == 0:
-                nc.scalar.activation(rows[u][:, :HALF], banks[0][:, :HALF], ACT.Relu, scale=0.0625)
-                nc.vector.tensor_scalar(rows[u][:, HALF:N], banks[4][:, HALF:], 0.0625, 0.0, ALU.mult, ALU.max)
+                nc.vector.tensor_scalar(rows[u][:, :HALF], moment_at(u, 0), 0.0625, 0.0, ALU.mult, ALU.max)
+                nc.scalar.activation(rows[u][:, HALF:N], moment_at(u, 1), ACT.Relu, scale=0.0625)
             else:
                 nc.scalar.activation(rows[u][:, :N], banks[u][:], ACT.Relu, scale=0.0625)
 
         def leave(u):
             if u == 0:
                 for h in range(2):
-                    cols = slice(h * HALF, (h + 1) * HALF)
-                    nc.scalar.activation(cv[:, u, cols], banks[4 * h][:, cols], ACT.Copy, scale=0.0625)
+                    nc.scalar.activation(cv[:, u, h * HALF : (h + 1) * HALF], moment_at(u, h), ACT.Copy, scale=0.0625)
             else:
                 nc.scalar.activation(cv[:, u, :], banks[u][:], ACT.Copy, scale=0.0625)
 

from contextlib import ExitStack

import concourse.mybir as mybir
from concourse.masks import make_identity

F32 = mybir.dt.float32
BF16 = mybir.dt.bfloat16
I32 = mybir.dt.int32
U32 = mybir.dt.uint32
U16 = mybir.dt.uint16
U8 = mybir.dt.uint8
FP8X4 = mybir.dt.float8_e4m3fn_x4
ALU = mybir.AluOpType
ACT = mybir.ActivationFunctionType

P = 128
PACK = 4
T, S, H, N, W, U = 2048, 512, 512, 512, 256, 1024
HALF = 256
RUN = 8
FLOPS = 3 * 2 * 512 * 512 * 512


def tile_picked_momfolddpagez_none_p_kernel(tc, x_words, x_scales, wa, wb, gt, gi, offs, two, n1, n2, n3, n4, n5, out):
    nc = tc.nc
    with ExitStack() as ctx:
        keep = ctx.enter_context(tc.tile_pool(name="keep", bufs=1))
        psum = ctx.enter_context(tc.psum_pool(name="psum", bufs=1))

        def sb(shape, dtype, name, tag=None):
            return keep.tile(shape, dtype, name=name, tag=tag or name, align_bytes=64)

        def load_list(src, name):
            tile = keep.tile(list(src.shape), U16, name=name)
            nc.sync.dma_start(tile[:], src)
            return tile

        def load_weight(src, c0, width, name):
            raw = sb([P, PACK, width], F32, name)
            nc.sync.dma_start(raw[:], src.rearrange("(p j) c -> p j c", j=PACK)[:, :, c0 : c0 + width])
            return raw

        def load_gate(src, queue, name):
            tile = sb([P, P], F32, name)
            nc.gpsimd.memset(tile[:], 0.0)
            queue.dma_start(
                tile[:PACK, :].rearrange("t (b i) -> t b i", i=RUN),
                src.rearrange("(b t i) o -> t b (i o)", t=PACK, i=RUN),
            )
            return tile

        xs = sb([P, T], U8, "xs")
        nc.vector.memset(xs[:].bitcast(I32), 0)
        gt_rows = load_gate(gt, nc.gpsimd, "gt_rows")
        ident = sb([P, P], F32, "ident")
        make_identity(nc, ident[:])

        offs_sb = load_list(offs, "offs_sb")
        wa_raw = [load_weight(wa, 0, HALF, "wa_raw0")]
        for q in range(4):
            nc.sync.dma_start(xs[32 * q : 32 * q + 4, :].bitcast(I32), x_scales[0, 4 * q : 4 * q + 4, :].bitcast(I32))
        two_sb = load_list(two, "two_sb")
        wa_raw.append(load_weight(wa, HALF, HALF, "wa_raw1"))
        xw = sb([P, T], I32, "xw")
        nc.sync.dma_start(xw[:], x_words[0].rearrange("p n t -> p (n t)").bitcast(I32))
        n1_sb = load_list(n1, "n1_sb")
        n2_sb = load_list(n2, "n2_sb")
        wb_raw = [load_weight(wb, c0, HALF, "wb_raw%d" % c0) for c0 in (0, HALF)]
        gi_rows = load_gate(gi, nc.sync, "gi_rows")
        n3_sb = load_list(n3, "n3_sb")
        n5_sb = load_list(n5, "n5_sb")
        n4_sb = load_list(n4, "n4_sb")

        rows = [sb([P, 2 * H], F32, "rows%d" % t) for t in range(PACK)]
        page = [sb([P, U], F32, "page%d" % t) for t in range(PACK)]
        for t in range(PACK):
            (nc.vector if t < 2 else nc.gpsimd).memset(page[t][:], 0.0)

        def pick_scales(lst, name):
            picked = sb([P, S], U8, name + "_picked")
            nc.vector.tensor_copy(picked[:], xs[:].indirect(lst[:]))
            dealt = sb([P, S], U8, name)
            return picked, dealt

        def deal_scales(picked, dealt):
            nc.vector.tensor_copy(
                dealt[:].bitcast(I32).rearrange("p (t b w) -> p t b w", t=PACK, w=RUN // 4),
                picked[:].bitcast(I32).rearrange("p (b t w) -> p t b w", t=PACK, w=RUN // 4),
            )

        def pick_words(lst, name):
            dealt = sb([P, PACK, P], U32, name)
            nc.vector.tensor_copy(dealt[:].rearrange("p t (b i) -> p b t i", i=RUN), xw[:].bitcast(U32).indirect(lst[:]))
            return dealt

        def cast_weight(raw, grouped):
            nc.scalar.copy(
                grouped.rearrange("p (c i) j -> p c j i", i=4),
                raw[:].rearrange("p j (c i) -> p c j i", i=4),
            )

        def quantize(grouped_ap, width, name, tag=None):
            codes = sb([P, width], U32, name + "_codes", tag)
            scales = sb([P, width], U8, name + "_scales")
            nc.vector.quantize_mx(out=codes[:].bitcast(FP8X4), scales=scales[:], in_=grouped_ap)
            return codes, scales

        def product(acc, lhs, rhs):
            nc.tensor.matmul_mx(
                out=acc,
                lhsT=lhs[0].bitcast(FP8X4),
                lhsT_scale=lhs[1],
                rhs=rhs[0].bitcast(FP8X4),
                rhs_scale=rhs[1],
                start=True,
                stop=True,
            )

        pa_s, xa_s = pick_scales(offs_sb, "xa_s")
        pb_s, xb_s = pick_scales(two_sb, "xb_s")
        deal_scales(pa_s, xa_s)
        deal_scales(pb_s, xb_s)

        wa_q = []
        for h in range(2):
            grouped = sb([P, HALF, PACK], BF16, "wa_bf%d" % h)
            cast_weight(wa_raw[h], grouped[:])
            wa_q.append(quantize(grouped[:].rearrange("p c j -> p (c j)"), HALF, "wa%d" % h))
        xa_w = pick_words(offs_sb, "xa_w")
        xb_w = pick_words(two_sb, "xb_w")

        banks = [psum.tile([P, 512], F32, name="bank%d" % i) for i in range(8)]

        def turn_gate(gate_rows, name):
            tile = sb([P, PACK], F32, name)
            nc.tensor.transpose(banks[7][:, :P], gate_rows[:], ident[:])
            nc.scalar.copy(tile[:], banks[7][:, :PACK])
            return tile

        gt_sb = turn_gate(gt_rows, "gt_sb")

        for t0 in (0, 2):
            for h in range(2):
                for t in (t0, t0 + 1):
                    acc = banks[2 * t + h][:, :HALF]
                    product(acc, (xa_w[:, t, :], xa_s[:, t * P : (t + 1) * P]), (wa_q[h][0][:], wa_q[h][1][:]))
                    nc.scalar.activation(rows[t][:, h * HALF : (h + 1) * HALF], acc, ACT.Copy, scale=gt_sb[:, t : t + 1])
        gi_sb = turn_gate(gi_rows, "gi_sb")

        twice = {}
        y = sb([P, PACK, H], F32, "y")
        pairs = {}

        def fetch_pairs(t):
            held = pairs[t // 2]
            nc.vector.tensor_copy(held[:, t % 2, 0, :], rows[t][:].indirect(n1_sb[:]))
            nc.vector.tensor_scalar(held[:, t % 2, 1, :], rows[t][:].indirect(n2_sb[:]), -0.5, 0.0, ALU.mult, ALU.add)

        def put_back(t):
            held = pairs[t // 2]
            nc.vector.tensor_tensor(rows[t][:].indirect(n2_sb[:]), held[:, t % 2, 0, :], held[:, t % 2, 1, :], ALU.add)

        def double(t):
            nc.scalar.activation(twice[t], rows[t][:, :H], ACT.Copy, scale=2.0)

        def fold(t):
            nc.vector.tensor_tensor(y[:, t, :], rows[t][:].indirect(n3_sb[:]), twice[t], ALU.subtract)

        def double_half(t, h):
            nc.scalar.activation(twice_last[h][:], rows[t][:, h * HALF : (h + 1) * HALF], ACT.Copy, scale=2.0)

        def fold_half(t, h):
            entries = n3_sb[:, h * HALF // 16 : (h + 1) * HALF // 16]
            nc.vector.tensor_tensor(
                y[:, t, h * HALF : (h + 1) * HALF], rows[t][:].indirect(entries), twice_last[h][:], ALU.subtract
            )

        z_bf = sb([P, PACK, P, PACK], BF16, "z_bf")
        z2_planes = sb([P, PACK, N], BF16, "z2_planes")
        z2_bf = sb([P, N, PACK], BF16, "z2_bf")

        wb_bf = sb([P, N, PACK], BF16, "wb_bf", "wa1_codes")
        for i in range(2):
            cast_weight(wb_raw[i], wb_bf[:, i * 256 : (i + 1) * 256, :])
        pairs[0] = sb([P, 2, 2, W], F32, "pairs0")[:]
        fetch_pairs(0)
        fetch_pairs(1)
        put_back(0)
        put_back(1)
        wb_q = quantize(wb_bf[:].rearrange("p c j -> p (c j)"), N, "wb")
        late = sb([P, 4 * H], F32, "late", "wb_raw256")
        twice[0], twice[1] = late[:, :H], late[:, H : 2 * H]
        twice[2] = sb([P, H], F32, "twice2")[:]
        twice_last = [sb([P, HALF], F32, "twice3_%d" % h) for h in range(2)]
        double(0)
        double(1)
        for t in range(PACK):
            product(banks[4 + t][:], (xb_w[:, t, :], xb_s[:, t * P : (t + 1) * P]), (wb_q[0][:], wb_q[1][:]))
            nc.scalar.activation(z2_planes[:, t, :], banks[4 + t][:], ACT.Copy, scale=gi_sb[:, t : t + 1])
        for h in range(2):
            nc.scalar.copy(
                z2_bf[:, h * 256 : (h + 1) * 256, :].rearrange("p (c i) t -> p c t i", i=4),
                z2_planes[:, :, h * 256 : (h + 1) * 256].rearrange("p t (c i) -> p c t i", i=4),
            )
        pairs[1] = late[:, 2 * H :].rearrange("p (t s w) -> p t s w", t=2, s=2)
        fetch_pairs(2)
        fold(0)
        fetch_pairs(3)
        put_back(2)
        double(2)
        fold(1)
        nc.scalar.activation(
            z_bf[:, :, :, 0:2].rearrange("p u m t -> p m u t"),
            y[:, 0:2, :].rearrange("p t (m u) -> p m u t", u=PACK),
            ACT.Copy,
            scale=-0.5,
        )
        put_back(3)
        double_half(3, 0)
        double_half(3, 1)
        fold(2)
        z2_q = []
        for h, done_with in ((0, "twice2"), (1, "twice3_0")):
            fold_half(3, h)
            z2_half = z2_bf[:, h * HALF : (h + 1) * HALF, :].rearrange("p n t -> p (n t)")
            z2_q.append(quantize(z2_half, HALF, "z2_%d" % h, done_with))

        cv = sb([P, PACK, N], F32, "cv")
        neg = sb([P, PACK, N], F32, "neg")
        out_rows = out.rearrange("(p u) w -> u p w", u=PACK)

        def moment_at(u, h):
            bank = banks[4] if (u, h) == (0, 1) else banks[u]
            return bank[:, h * HALF : (h + 1) * HALF]

        def moments(u):
            pieces = 2 if u < 2 else 1
            for h in range(pieces):
                ms = slice(h * P // pieces, (h + 1) * P // pieces)
                nc.scalar.activation(
                    z_bf[:, u, ms, 2:4],
                    y[:, 2:4, :].rearrange("p t (m u) -> p u m t", u=PACK)[:, u, ms, :],
                    ACT.Copy,
                    scale=-0.5,
                )
            z_q = quantize(z_bf[:, u, :, :].rearrange("p m t -> p (m t)"), P, "zblock%d" % u)
            for h in range(2):
                product(moment_at(u, h), (z_q[0][:], z_q[1][:]), (z2_q[h][0][:], z2_q[h][1][:]))

        def positive(u):
            if u == 0:
                nc.vector.tensor_scalar(rows[u][:, :HALF], moment_at(u, 0), 0.0625, 0.0, ALU.mult, ALU.max)
                nc.scalar.activation(rows[u][:, HALF:N], moment_at(u, 1), ACT.Relu, scale=0.0625)
            else:
                nc.scalar.activation(rows[u][:, :N], banks[u][:], ACT.Relu, scale=0.0625)

        def leave(u):
            if u == 0:
                for h in range(2):
                    nc.scalar.activation(cv[:, u, h * HALF : (h + 1) * HALF], moment_at(u, h), ACT.Copy, scale=0.0625)
            else:
                nc.scalar.activation(cv[:, u, :], banks[u][:], ACT.Copy, scale=0.0625)

        def fetch_relu(u):
            nc.vector.tensor_scalar(neg[:, u, :], rows[u][:].indirect(n5_sb[:]), -1.0, 0.0, ALU.mult, ALU.add)

        def put_page(u):
            nc.vector.tensor_tensor(page[u][:].indirect(n4_sb[:]), cv[:, u, :], neg[:, u, :], ALU.add)
            nc.sync.dma_start(out_rows[u], page[u][:])

        moments(0)
        moments(1)
        positive(0)
        fetch_relu(0)
        for u in range(PACK):
            if u + 1 < PACK:
                positive(u + 1)
                fetch_relu(u + 1)
            if u + 2 < PACK:
                moments(u + 2)
            leave(u)
            put_page(u)
